import numpy as np
import ml_dtypes


def mxq(x, axis, fmt="e4m3"):
    dtype, down = {"e4m3": (ml_dtypes.float8_e4m3fn, 7), "e5m2": (ml_dtypes.float8_e5m2, 14)}[fmt]
    v = np.moveaxis(np.asarray(x, np.float32).astype(ml_dtypes.bfloat16).astype(np.float64), axis, -1)
    blocks = v.reshape(v.shape[:-1] + (-1, 32))
    amax = np.abs(blocks).max(-1, keepdims=True)
    byte = np.maximum(np.where(amax > 0, np.frexp(amax)[1] - 1 + 127, 0) - down, 1)
    scale = np.exp2(byte - 127.0)
    codes = (blocks / scale).astype(np.float32).astype(dtype).astype(np.float64)
    return np.moveaxis((codes * scale).reshape(v.shape), -1, axis)


WIDE = False


def mx_kscale(k):
    if not WIDE:
        return np.ones(k)
    levels = np.array([10, -10, 5, -5, 0])
    if k % 512:
        return np.exp2(np.random.permutation(np.resize(levels, k // 32))).repeat(32)
    a = np.empty((k // 512, 16))
    for p in range(k // 512):
        a[p, :8] = np.random.permutation(np.resize(levels, 8))
        for g in range(8):
            far = levels[np.abs(levels - a[p, g]) >= 10]
            a[p, g + 8] = far[np.random.randint(len(far))]
    return np.exp2(a.ravel()).repeat(32)


def f64(x):
    return np.asarray(x).astype(np.float64)


def striped(idx):
    return np.tile(np.asarray(idx).reshape(-1, 16).T, (8, 1)).astype(np.uint16)


def unstriped(offs):
    return offs[:16].T.reshape(-1).astype(np.int64)


E2M1 = np.array([0.0, 0.5, 1.0, 1.5, 2.0, 3.0, 4.0, 6.0, -0.0, -0.5, -1.0, -1.5, -2.0, -3.0, -4.0, -6.0])


def pack_weight(w, fmt):
    k, n = w.shape
    w = f64(np.asarray(w, np.float32).astype(ml_dtypes.bfloat16)).reshape(k // 32, 32, n)
    amax = np.abs(w).max(1)
    if fmt == "e4m3":
        byte = np.frexp(amax)[1] - 1 + 127 - 7
    else:
        mant, ex = np.frexp(amax / 6.0)
        byte = np.where(mant > 0.5, ex, ex - 1) + 127
    byte = np.clip(np.where(amax > 0, byte, 1), 1, 254)
    scaled = (w * np.exp2(127.0 - byte)[:, None, :]).reshape(k, n).astype(np.float32)
    by_word = np.ascontiguousarray(scaled.reshape(k // 512, 128, 4, n).transpose(0, 1, 3, 2))
    if fmt == "e4m3":
        words = by_word.astype(ml_dtypes.float8_e4m3fn).view(np.uint8)
    else:
        c = by_word.astype(ml_dtypes.float4_e2m1fn).view(np.uint8) & 0xF
        words = (c[..., 0::2] | (c[..., 1::2] << 4)).reshape(k // 512, 128, 2 * n)
    return np.ascontiguousarray(words), np.ascontiguousarray(byte.astype(np.uint8).reshape(k // 512, 16, n))


def unpack_weight(words, scales, fmt):
    g, _, n = scales.shape
    words = np.ascontiguousarray(words).reshape(g, 128, n, -1)
    if fmt == "e4m3":
        vals = words.view(ml_dtypes.float8_e4m3fn).astype(np.float64)
    else:
        nib = np.empty((g, 128, n, 4), np.uint8)
        nib[..., 0::2] = words & 0xF
        nib[..., 1::2] = words >> 4
        vals = E2M1[nib]
    vals = vals * np.repeat(np.exp2(scales.astype(np.float64) - 127.0), 8, axis=1)[..., None]
    return vals.transpose(0, 1, 3, 2).reshape(g * 512, n)


def bf(x):
    return np.asarray(x, np.float32).astype(ml_dtypes.bfloat16)


def planes(Y):
    r, m = Y.shape
    b = f64(bf(Y)).reshape(r // 32, 32, m)
    amax = np.abs(b).max(1)
    byte = np.clip(np.where(amax > 0, np.frexp(amax)[1] - 1 + 127 - 7, 1), 1, 254)
    codes = (b * np.exp2(127.0 - byte)[:, None, :]).reshape(r, m).astype(np.float32).astype(ml_dtypes.float8_e4m3fn).view(np.uint8)
    words = codes.reshape(r // 512, 128, 4, m).transpose(0, 1, 3, 2)
    return np.ascontiguousarray(words), np.ascontiguousarray(byte.astype(np.uint8).reshape(r // 512, 16, m))


K, T, J, I, R, S, L, N = 1024, 2048, 512, 256, 512, 512, 512, 512


def setup_inputs():
    n = np.random.standard_normal
    idx = np.random.permutation(T)[:J]
    idx2 = np.random.permutation(J)[:I]
    idx3 = np.random.randint(0, I, S)
    fk = mx_kscale(K)
    fr = mx_kscale(R)
    fl = mx_kscale(L)
    xtp = pack_weight(n((K, T)) / fk[:, None], "e2m1")
    wap = pack_weight(n((K, R)) * 1 / np.sqrt(K) * fk[:, None] * fr, "e4m3")
    wbp = pack_weight(n((R, N)) * 1 / np.sqrt(R) / fr[:, None], "e2m1")
    rdp = pack_weight(n((L, S)) / fl[:, None], "e4m3")
    wrp = pack_weight(n((L, N)) * 1 / np.sqrt(L) * fl[:, None], "e2m1")
    return {
        "xt_words": xtp[0],
        "xt_scales": xtp[1],
        "wa_words": wap[0],
        "wa_scales": wap[1],
        "wb_words": wbp[0],
        "wb_scales": wbp[1],
        "rd_words": rdp[0],
        "rd_scales": rdp[1],
        "wr_words": wrp[0],
        "wr_scales": wrp[1],
        "offs": striped(idx),
        "offs2": striped(idx2),
        "offs3": striped(idx3),
    }


def reference(xt_words, xt_scales, wa_words, wa_scales, wb_words, wb_scales, rd_words, rd_scales, wr_words, wr_scales, offs, offs2, offs3):
    idx = unstriped(offs)
    idx2 = unstriped(offs2)
    idx3 = unstriped(offs3)
    xtu = unpack_weight(xt_words, xt_scales, "e2m1")
    wau = unpack_weight(wa_words, wa_scales, "e4m3")
    wbu = unpack_weight(wb_words, wb_scales, "e2m1")
    rdu = unpack_weight(rd_words, rd_scales, "e4m3")
    wru = unpack_weight(wr_words, wr_scales, "e2m1")
    xtidxg = xtu[:, idx]
    a = wau.T @ xtidxg
    hid = np.maximum(a, 0.0)
    hididx2q = mxq(hid[:, idx2], 0, "e4m3")
    p = wbu.T @ hididx2q
    q = wru.T @ rdu
    y = p[:, idx3] * q
    words, scales = planes(y)
    return y, words, scales

@@ -1,0 +1,216 @@
+from contextlib import ExitStack
+
+import concourse.mybir as mybir
+
+K, T, J, I, R, S, L, N = 1024, 2048, 512, 256, 512, 512, 512, 512
+FLOPS = 2 * (K * R * J + R * N * I + L * N * S)
+
+F32 = mybir.dt.float32
+BF16 = mybir.dt.bfloat16
+I32 = mybir.dt.int32
+U32 = mybir.dt.uint32
+U16 = mybir.dt.uint16
+U8 = mybir.dt.uint8
+E4M3X4 = mybir.dt.float8_e4m3fn_x4
+E2M1X4 = mybir.dt.float4_e2m1fn_x4
+ACT = mybir.ActivationFunctionType
+MULT = mybir.AluOpType.mult
+
+P = 128
+PACK = 4
+HALF = 256
+SPARE = 16
+
+
+def dealt(ap, run):
+    return ap.rearrange("p (t b m) -> p b t m", t=PACK, m=run)
+
+
+def undealt(ap, run):
+    return ap.rearrange("p (b m t) -> p b t m", t=PACK, m=run)
+
+
+def tile_list_three_list_relay_pl_kernel(
+    tc, xt_words, xt_scales, wa_words, wa_scales, wb_words, wb_scales, rd_words, rd_scales,
+    wr_words, wr_scales, offs, offs2, offs3, out_0, out_1, out_2,
+):
+    nc = tc.nc
+    with ExitStack() as ctx:
+        sb = ctx.enter_context(tc.tile_pool(name="sb", bufs=1))
+        ps = ctx.enter_context(tc.psum_pool(name="ps", bufs=1))
+
+        def tile(shape, dtype, name):
+            return sb.tile(shape, dtype, name=name, align_bytes=64)
+
+        def load_scale_rows(queue, plane, scales):
+            for q in range(4):
+                queue.dma_start(
+                    plane[32 * q : 32 * q + 4, :, :].bitcast(I32),
+                    scales[:, 4 * q : 4 * q + 4, :].rearrange("z r c -> r z c").bitcast(I32),
+                )
+
+        list1 = sb.tile([P, J // 16], U16, name="list1")
+        list2 = sb.tile([P, I // 16], U16, name="list2")
+        list3 = sb.tile([P, S // 16], U16, name="list3")
+        xw = [tile([P, T], U16, f"xw{z}") for z in range(2)]
+        xs = tile([P, 2, T], U8, "xs")
+        wa_raw = [tile([P, R], U32, f"wa_raw{z}") for z in range(2)]
+        was_raw = tile([P, 2, R], U8, "was_raw")
+        rd = tile([P, S], U32, "rd")
+        rds = tile([P, 1, S], U8, "rds")
+        wr_raw = tile([P, N], U16, "wr_raw")
+        wrs_raw = tile([P, 1, N], U8, "wrs_raw")
+        wb_raw = tile([P, N], U16, "wb_raw")
+        wbs_raw = tile([P, 1, N], U8, "wbs_raw")
+        pwin = [tile([P, I + SPARE], F32, f"pwin{t}") for t in range(PACK)]
+
+        nc.gpsimd.memset(was_raw[:].bitcast(I32), 0)
+        nc.vector.memset(xs[:].bitcast(I32), 0)
+        for plane in (wrs_raw, rds, wbs_raw):
+            nc.gpsimd.memset(plane[:].bitcast(I32), 0)
+        for t in range(PACK):
+            nc.gpsimd.memset(pwin[t][:, I:], 0.0)
+
+        nc.sync.dma_start(list1[:], offs)
+        load_scale_rows(nc.sync, was_raw, wa_scales)
+        nc.sync.dma_start(xw[0][:].bitcast(I32), xt_words[0].bitcast(I32))
+        nc.sync.dma_start(wa_raw[0][:].bitcast(I32), wa_words[0].rearrange("p c r -> p (c r)").bitcast(I32))
+        load_scale_rows(nc.sync, xs, xt_scales)
+        nc.sync.dma_start(xw[1][:].bitcast(I32), xt_words[1].bitcast(I32))
+        nc.sync.dma_start(wa_raw[1][:].bitcast(I32), wa_words[1].rearrange("p c r -> p (c r)").bitcast(I32))
+        nc.sync.dma_start(wr_raw[:].bitcast(I32), wr_words[0].bitcast(I32))
+        nc.sync.dma_start(list2[:], offs2)
+        load_scale_rows(nc.sync, wrs_raw, wr_scales)
+        nc.sync.dma_start(rd[:].bitcast(I32), rd_words[0].rearrange("p c r -> p (c r)").bitcast(I32))
+        load_scale_rows(nc.sync, rds, rd_scales)
+        nc.sync.dma_start(wb_raw[:].bitcast(I32), wb_words[0].bitcast(I32))
+        load_scale_rows(nc.sync, wbs_raw, wb_scales)
+        nc.sync.dma_start(list3[:], offs3)
+
+        wa = [tile([P, R], U32, f"wa{z}") for z in range(2)]
+        was = [tile([P, R], U8, f"was{z}") for z in range(2)]
+        xg = [[tile([P, HALF], U16, f"xg{z}{h}") for h in range(2)] for z in range(2)]
+        sg = [[tile([P, HALF], U8, f"sg{z}{h}") for h in range(2)] for z in range(2)]
+        cols = HALF // 16
+        for h in range(2):
+            nc.vector.tensor_copy(xg[0][h][:], xw[0][:].indirect(list1[:, h * cols : (h + 1) * cols]))
+        for z in range(2):
+            nc.vector.tensor_copy(dealt(was[z][:], 16), undealt(was_raw[:, z, :], 16))
+            nc.scalar.copy(dealt(wa[z][:], 4), undealt(wa_raw[z][:], 4))
+        for z in range(2):
+            for h in range(2):
+                nc.vector.tensor_copy(sg[z][h][:], xs[:, z, :].indirect(list1[:, h * cols : (h + 1) * cols]))
+        for h in range(2):
+            nc.vector.tensor_copy(xg[1][h][:], xw[1][:].indirect(list1[:, h * cols : (h + 1) * cols]))
+
+        order = (0, 2, 1, 3)
+        a_ps = [[ps.tile([P, HALF], F32, name=f"a{h}{t}", tag=f"bank{h}{t}") for t in range(PACK)] for h in range(2)]
+        hid = [tile([P, J], F32, f"hid{t}") for t in range(PACK)]
+        for z in range(2):
+            for h in range(2):
+                for t in order:
+                    nc.tensor.matmul_mx(
+                        a_ps[h][t][:],
+                        lhsT=wa[z][:, t * P : (t + 1) * P].bitcast(E4M3X4),
+                        lhsT_scale=was[z][:, t * P : (t + 1) * P],
+                        rhs=xg[z][h][:].bitcast(E2M1X4),
+                        rhs_scale=sg[z][h][:],
+                        start=(z == 0),
+                        stop=(z == 1),
+                    )
+        wr = tile([P, N], U16, "wr")
+        wrs = tile([P, N], U8, "wrs")
+        wb = tile([P, N], U16, "wb")
+        wbs = tile([P, N], U8, "wbs")
+        nc.scalar.copy(dealt(wr[:], 8), undealt(wr_raw[:], 8))
+        for t in order:
+            nc.scalar.activation(hid[t][:, :HALF], a_ps[0][t][:], ACT.Relu)
+        nc.vector.tensor_copy(dealt(wrs[:], 16), undealt(wrs_raw[:, 0, :], 16))
+        for t in order:
+            if t < 2:
+                nc.scalar.activation(hid[t][:, HALF:], a_ps[1][t][:], ACT.Relu)
+            else:
+                nc.vector.tensor_scalar_max(hid[t][:, HALF:], a_ps[1][t][:], 0.0)
+
+        q_ps = [ps.tile([P, S], F32, name=f"q{t}", tag=f"bank1{t}") for t in range(PACK)]
+        for t in order:
+            nc.tensor.matmul_mx(
+                q_ps[t][:],
+                lhsT=wr[:, t * P : (t + 1) * P].bitcast(E2M1X4),
+                lhsT_scale=wrs[:, t * P : (t + 1) * P],
+                rhs=rd[:].bitcast(E4M3X4),
+                rhs_scale=rds[:, 0, :],
+                start=True,
+                stop=True,
+            )
+
+        hg = tile([P, PACK, I], F32, "hg")
+        for t in order:
+            if t < 2:
+                nc.scalar.activation(hg[:, t, :], hid[t][:].indirect(list2[:]), ACT.Copy)
+            else:
+                nc.vector.tensor_copy(hg[:, t, :], hid[t][:].indirect(list2[:]))
+        nc.scalar.copy(dealt(wb[:], 8), undealt(wb_raw[:], 8))
+        nc.vector.tensor_copy(dealt(wbs[:], 16), undealt(wbs_raw[:, 0, :], 16))
+        hb = tile([P, I, PACK], BF16, "hb")
+        nc.vector.tensor_copy(
+            hb[:].rearrange("p (c i) t -> p c t i", i=4), hg[:].rearrange("p t (c i) -> p c t i", i=4)
+        )
+        hq = tile([P, I], U32, "hq")
+        hqs = tile([P, I], U8, "hqs")
+        nc.vector.quantize_mx(hq[:].bitcast(E4M3X4), hqs[:], hb[:].rearrange("p c t -> p (c t)"))
+        p_ps = [ps.tile([P, I], F32, name=f"p{t}", tag=f"bank0{t}") for t in range(PACK)]
+        for t in range(PACK):
+            nc.tensor.matmul_mx(
+                p_ps[t][:],
+                lhsT=wb[:, t * P : (t + 1) * P].bitcast(E2M1X4),
+                lhsT_scale=wbs[:, t * P : (t + 1) * P],
+                rhs=hq[:].bitcast(E4M3X4),
+                rhs_scale=hqs[:],
+                start=True,
+                stop=True,
+            )
+        for t in range(PACK):
+            if t % 2 == 0:
+                nc.scalar.copy(pwin[t][:, :I], p_ps[t][:])
+            else:
+                nc.vector.tensor_copy(pwin[t][:, :I], p_ps[t][:])
+
+        y_rows = out_0.rearrange("(p t) s -> p t s", t=PACK)
+        codes = out_1[0].rearrange("p c r -> p (c r)").bitcast(I32)
+        yq = tile([P, S], U32, "yq")
+        yqs = tile([P, S], U8, "yqs")
+        chunks = ((0, 256, (1,)), (256, 128, ()), (384, 128, (1, 3)))
+        pending = []
+        for first, width, on_vector in chunks:
+            span = slice(first, first + width)
+            entries = list3[:, first // 16 : (first + width) // 16]
+            y = tile([P, PACK, width], F32, f"y{first}")
+            pg = [tile([P, width], F32, f"pg{first}_{t}") for t in range(PACK)]
+            for t in range(PACK):
+                if t in on_vector:
+                    nc.vector.tensor_copy(pg[t][:], pwin[t][:].indirect(entries))
+                else:
+                    nc.scalar.activation(pg[t][:], pwin[t][:].indirect(entries), ACT.Copy)
+            for t in range(PACK):
+                nc.vector.tensor_tensor(y[:, t, :], pg[t][:], q_ps[t][:, span], MULT)
+                if t == 0:
+                    for step in pending:
+                        step()
+                    pending.clear()
+            nc.sync.dma_start(y_rows[:, :, span], y[:])
+            yb = tile([P, width, PACK], BF16, f"yb{first}")
+            nc.vector.tensor_copy(
+                yb[:].rearrange("p (c i) t -> p c t i", i=4), y[:].rearrange("p t (c i) -> p c t i", i=4)
+            )
+
+            def quantise(span=span, yb=yb):
+                nc.vector.quantize_mx(yq[:, span].bitcast(E4M3X4), yqs[:, span], yb[:].rearrange("p c t -> p (c t)"))
+                nc.sync.dma_start(codes[:, span], yq[:, span].bitcast(I32))
+
+            pending.append(quantise)
+        for step in pending:
+            step()
+        for q in range(4):
+            queue = nc.sync if q % 2 == 0 else nc.scalar
+            queue.dma_start(out_2[0, 4 * q : 4 * q + 4, :].bitcast(I32), yqs[32 * q : 32 * q + 4, :].bitcast(I32))

@@ -53,7 +53,7 @@ def tile_list_three_list_relay_pl_kernel(
         list2 = sb.tile([P, I // 16], U16, name="list2")
         list3 = sb.tile([P, S // 16], U16, name="list3")
         xw = [tile([P, T], U16, f"xw{z}") for z in range(2)]
-        xs = tile([P, 2, T], U8, "xs")
+        xs = tile([P, T], U8, "xs")
         wa_raw = [tile([P, R], U32, f"wa_raw{z}") for z in range(2)]
         was_raw = tile([P, 2, R], U8, "was_raw")
         rd = tile([P, S], U32, "rd")
@@ -64,44 +64,46 @@ def tile_list_three_list_relay_pl_kernel(
         wbs_raw = tile([P, 1, N], U8, "wbs_raw")
         pwin = [tile([P, I + SPARE], F32, f"pwin{t}") for t in range(PACK)]
 
-        nc.gpsimd.memset(was_raw[:].bitcast(I32), 0)
-        nc.vector.memset(xs[:].bitcast(I32), 0)
-        for plane in (wrs_raw, rds, wbs_raw):
+        sg = [tile([P, J], U8, f"sg{z}") for z in range(2)]
+        nc.gpsimd.memset(xs[:].bitcast(I32), 0)
+        for plane in (was_raw, wrs_raw, rds, wbs_raw):
             nc.gpsimd.memset(plane[:].bitcast(I32), 0)
+        nc.gpsimd.memset(sg[1][:].bitcast(I32), 0)
+        zeros = tile([P, SPARE], F32, "zeros")
+        nc.vector.memset(zeros[:], 0.0)
         for t in range(PACK):
-            nc.gpsimd.memset(pwin[t][:, I:], 0.0)
+            nc.scalar.copy(pwin[t][:, I:], zeros[:])
 
         nc.sync.dma_start(list1[:], offs)
-        load_scale_rows(nc.sync, was_raw, wa_scales)
+        nc.sync.dma_start(list2[:], offs2)
+        xs_rows = xt_scales.rearrange("z (q r) c -> r q z c", r=4).bitcast(I32)
+        for r in range(4):
+            nc.sync.dma_start(xs[r:P:16, :].bitcast(I32), xs_rows[r])
         nc.sync.dma_start(xw[0][:].bitcast(I32), xt_words[0].bitcast(I32))
         nc.sync.dma_start(wa_raw[0][:].bitcast(I32), wa_words[0].rearrange("p c r -> p (c r)").bitcast(I32))
-        load_scale_rows(nc.sync, xs, xt_scales)
+        load_scale_rows(nc.sync, was_raw, wa_scales)
         nc.sync.dma_start(xw[1][:].bitcast(I32), xt_words[1].bitcast(I32))
         nc.sync.dma_start(wa_raw[1][:].bitcast(I32), wa_words[1].rearrange("p c r -> p (c r)").bitcast(I32))
         nc.sync.dma_start(wr_raw[:].bitcast(I32), wr_words[0].bitcast(I32))
-        nc.sync.dma_start(list2[:], offs2)
-        load_scale_rows(nc.sync, wrs_raw, wr_scales)
-        nc.sync.dma_start(rd[:].bitcast(I32), rd_words[0].rearrange("p c r -> p (c r)").bitcast(I32))
-        load_scale_rows(nc.sync, rds, rd_scales)
         nc.sync.dma_start(wb_raw[:].bitcast(I32), wb_words[0].bitcast(I32))
+        nc.sync.dma_start(rd[:].bitcast(I32), rd_words[0].rearrange("p c r -> p (c r)").bitcast(I32))
+        load_scale_rows(nc.gpsimd, wrs_raw, wr_scales)
+        load_scale_rows(nc.sync, rds, rd_scales)
         load_scale_rows(nc.sync, wbs_raw, wb_scales)
         nc.sync.dma_start(list3[:], offs3)
 
         wa = [tile([P, R], U32, f"wa{z}") for z in range(2)]
         was = [tile([P, R], U8, f"was{z}") for z in range(2)]
         xg = [[tile([P, HALF], U16, f"xg{z}{h}") for h in range(2)] for z in range(2)]
-        sg = [[tile([P, HALF], U8, f"sg{z}{h}") for h in range(2)] for z in range(2)]
         cols = HALF // 16
-        for h in range(2):
-            nc.vector.tensor_copy(xg[0][h][:], xw[0][:].indirect(list1[:, h * cols : (h + 1) * cols]))
+        nc.vector.tensor_copy(sg[0][:], xs[:].indirect(list1[:]))
+        nc.scalar.dma_start(sg[1][0:112, :].bitcast(I32), sg[0][16:P, :].bitcast(I32))
         for z in range(2):
-            nc.vector.tensor_copy(dealt(was[z][:], 16), undealt(was_raw[:, z, :], 16))
             nc.scalar.copy(dealt(wa[z][:], 4), undealt(wa_raw[z][:], 4))
-        for z in range(2):
             for h in range(2):
-                nc.vector.tensor_copy(sg[z][h][:], xs[:, z, :].indirect(list1[:, h * cols : (h + 1) * cols]))
-        for h in range(2):
-            nc.vector.tensor_copy(xg[1][h][:], xw[1][:].indirect(list1[:, h * cols : (h + 1) * cols]))
+                nc.vector.tensor_copy(xg[z][h][:], xw[z][:].indirect(list1[:, h * cols : (h + 1) * cols]))
+                if z == 0:
+                    nc.vector.tensor_copy(dealt(was[h][:], 16), undealt(was_raw[:, h, :], 16))
 
         order = (0, 2, 1, 3)
         a_ps = [[ps.tile([P, HALF], F32, name=f"a{h}{t}", tag=f"bank{h}{t}") for t in range(PACK)] for h in range(2)]
@@ -114,7 +116,7 @@ def tile_list_three_list_relay_pl_kernel(
                         lhsT=wa[z][:, t * P : (t + 1) * P].bitcast(E4M3X4),
                         lhsT_scale=was[z][:, t * P : (t + 1) * P],
                         rhs=xg[z][h][:].bitcast(E2M1X4),
-                        rhs_scale=sg[z][h][:],
+                        rhs_scale=sg[z][:, h * HALF : (h + 1) * HALF],
                         start=(z == 0),
                         stop=(z == 1),
                     )
@@ -123,14 +125,16 @@ def tile_list_three_list_relay_pl_kernel(
         wb = tile([P, N], U16, "wb")
         wbs = tile([P, N], U8, "wbs")
         nc.scalar.copy(dealt(wr[:], 8), undealt(wr_raw[:], 8))
-        for t in order:
-            nc.scalar.activation(hid[t][:, :HALF], a_ps[0][t][:], ACT.Relu)
-        nc.vector.tensor_copy(dealt(wrs[:], 16), undealt(wrs_raw[:, 0, :], 16))
-        for t in order:
-            if t < 2:
-                nc.scalar.activation(hid[t][:, HALF:], a_ps[1][t][:], ACT.Relu)
-            else:
-                nc.vector.tensor_scalar_max(hid[t][:, HALF:], a_ps[1][t][:], 0.0)
+        nc.scalar.copy(dealt(wb[:], 8), undealt(wb_raw[:], 8))
+        nc.gpsimd.tensor_copy(dealt(wrs[:], 16), undealt(wrs_raw[:, 0, :], 16))
+        nc.gpsimd.tensor_copy(dealt(wbs[:], 16), undealt(wbs_raw[:, 0, :], 16))
+        for h in range(2):
+            for t in order:
+                part = hid[t][:, h * HALF : (h + 1) * HALF]
+                if t < 2:
+                    nc.scalar.activation(part, a_ps[h][t][:], ACT.Relu)
+                else:
+                    nc.vector.tensor_scalar_max(part, a_ps[h][t][:], 0.0)
 
         q_ps = [ps.tile([P, S], F32, name=f"q{t}", tag=f"bank1{t}") for t in range(PACK)]
         for t in order:
@@ -150,12 +154,12 @@ def tile_list_three_list_relay_pl_kernel(
                 nc.scalar.activation(hg[:, t, :], hid[t][:].indirect(list2[:]), ACT.Copy)
             else:
                 nc.vector.tensor_copy(hg[:, t, :], hid[t][:].indirect(list2[:]))
-        nc.scalar.copy(dealt(wb[:], 8), undealt(wb_raw[:], 8))
-        nc.vector.tensor_copy(dealt(wbs[:], 16), undealt(wbs_raw[:, 0, :], 16))
         hb = tile([P, I, PACK], BF16, "hb")
-        nc.vector.tensor_copy(
-            hb[:].rearrange("p (c i) t -> p c t i", i=4), hg[:].rearrange("p t (c i) -> p c t i", i=4)
-        )
+        for copy, part in ((nc.vector.tensor_copy, slice(0, 176)), (nc.scalar.copy, slice(176, I))):
+            copy(
+                hb[:, part, :].rearrange("p (c i) t -> p c t i", i=4),
+                hg[:, :, part].rearrange("p t (c i) -> p c t i", i=4),
+            )
         hq = tile([P, I], U32, "hq")
         hqs = tile([P, I], U8, "hqs")
         nc.vector.quantize_mx(hq[:].bitcast(E4M3X4), hqs[:], hb[:].rearrange("p c t -> p (c t)"))
@@ -180,7 +184,7 @@ def tile_list_three_list_relay_pl_kernel(
         codes = out_1[0].rearrange("p c r -> p (c r)").bitcast(I32)
         yq = tile([P, S], U32, "yq")
         yqs = tile([P, S], U8, "yqs")
-        chunks = ((0, 256, (1,)), (256, 128, ()), (384, 128, (1, 3)))
+        chunks = ((0, 256, (1,)), (256, 128, ()), (384, 128, ()))
         pending = []
         for first, width, on_vector in chunks:
             span = slice(first, first + width)

@@ -18,16 +18,29 @@ MULT = mybir.AluOpType.mult
 
 P = 128
 PACK = 4
-HALF = 256
+PASSES = K // (P * PACK)
+QUADRANTS = 4
+ENTRIES = 16
+LINE = 16
+HALF = J // 2
 SPARE = 16
+SHIFT = 16
+SLICE_ORDER = (0, 2, 1, 3)
+SCALAR_SLICES = (0, 1)
+VECTOR_COLUMNS = 176
+CHUNKS = ((0, 256, (1,)), (256, 128, ()), (384, 128, ()))
 
 
-def dealt(ap, run):
-    return ap.rearrange("p (t b m) -> p b t m", t=PACK, m=run)
+def deal(copy, dealt, raw, element_bytes):
+    run = LINE // element_bytes
+    copy(
+        dealt.rearrange("p (t b m) -> p b t m", t=PACK, m=run),
+        raw.rearrange("p (b m t) -> p b t m", t=PACK, m=run),
+    )
 
 
-def undealt(ap, run):
-    return ap.rearrange("p (b m t) -> p b t m", t=PACK, m=run)
+def interleave(copy, words, slices):
+    copy(words.rearrange("p (c i) t -> p c t i", i=4), slices.rearrange("p t (c i) -> p c t i", i=4))
 
 
 def tile_list_three_list_relay_pl_kernel(
@@ -42,20 +55,20 @@ def tile_list_three_list_relay_pl_kernel(
         def tile(shape, dtype, name):
             return sb.tile(shape, dtype, name=name, align_bytes=64)
 
-        def load_scale_rows(queue, plane, scales):
-            for q in range(4):
+        def load_scale_rows(queue, rows, scales):
+            for q in range(QUADRANTS):
                 queue.dma_start(
-                    plane[32 * q : 32 * q + 4, :, :].bitcast(I32),
+                    rows[32 * q : 32 * q + 4, :, :].bitcast(I32),
                     scales[:, 4 * q : 4 * q + 4, :].rearrange("z r c -> r z c").bitcast(I32),
                 )
 
-        list1 = sb.tile([P, J // 16], U16, name="list1")
-        list2 = sb.tile([P, I // 16], U16, name="list2")
-        list3 = sb.tile([P, S // 16], U16, name="list3")
-        xw = [tile([P, T], U16, f"xw{z}") for z in range(2)]
+        list1 = sb.tile([P, J // ENTRIES], U16, name="list1")
+        list2 = sb.tile([P, I // ENTRIES], U16, name="list2")
+        list3 = sb.tile([P, S // ENTRIES], U16, name="list3")
+        xw = [tile([P, T], U16, f"xw{z}") for z in range(PASSES)]
         xs = tile([P, T], U8, "xs")
-        wa_raw = [tile([P, R], U32, f"wa_raw{z}") for z in range(2)]
-        was_raw = tile([P, 2, R], U8, "was_raw")
+        wa_raw = [tile([P, R], U32, f"wa_raw{z}") for z in range(PASSES)]
+        was_raw = tile([P, PASSES, R], U8, "was_raw")
         rd = tile([P, S], U32, "rd")
         rds = tile([P, 1, S], U8, "rds")
         wr_raw = tile([P, N], U16, "wr_raw")
@@ -64,10 +77,10 @@ def tile_list_three_list_relay_pl_kernel(
         wbs_raw = tile([P, 1, N], U8, "wbs_raw")
         pwin = [tile([P, I + SPARE], F32, f"pwin{t}") for t in range(PACK)]
 
-        sg = [tile([P, J], U8, f"sg{z}") for z in range(2)]
+        sg = [tile([P, J], U8, f"sg{z}") for z in range(PASSES)]
         nc.gpsimd.memset(xs[:].bitcast(I32), 0)
-        for plane in (was_raw, wrs_raw, rds, wbs_raw):
-            nc.gpsimd.memset(plane[:].bitcast(I32), 0)
+        for rows in (was_raw, wrs_raw, rds, wbs_raw):
+            nc.gpsimd.memset(rows[:].bitcast(I32), 0)
         nc.gpsimd.memset(sg[1][:].bitcast(I32), 0)
         zeros = tile([P, SPARE], F32, "zeros")
         nc.vector.memset(zeros[:], 0.0)
@@ -78,7 +91,7 @@ def tile_list_three_list_relay_pl_kernel(
         nc.sync.dma_start(list2[:], offs2)
         xs_rows = xt_scales.rearrange("z (q r) c -> r q z c", r=4).bitcast(I32)
         for r in range(4):
-            nc.sync.dma_start(xs[r:P:16, :].bitcast(I32), xs_rows[r])
+            nc.sync.dma_start(xs[r:P:SHIFT, :].bitcast(I32), xs_rows[r])
         nc.sync.dma_start(xw[0][:].bitcast(I32), xt_words[0].bitcast(I32))
         nc.sync.dma_start(wa_raw[0][:].bitcast(I32), wa_words[0].rearrange("p c r -> p (c r)").bitcast(I32))
         load_scale_rows(nc.sync, was_raw, wa_scales)
@@ -86,31 +99,32 @@ def tile_list_three_list_relay_pl_kernel(
         nc.sync.dma_start(wa_raw[1][:].bitcast(I32), wa_words[1].rearrange("p c r -> p (c r)").bitcast(I32))
         nc.sync.dma_start(wr_raw[:].bitcast(I32), wr_words[0].bitcast(I32))
         nc.sync.dma_start(wb_raw[:].bitcast(I32), wb_words[0].bitcast(I32))
+        nc.vector.tensor_copy(sg[0][:], xs[:].indirect(list1[:]))
+        nc.sync.dma_start(sg[1][0 : P - SHIFT, :].bitcast(I32), sg[0][SHIFT:P, :].bitcast(I32))
         nc.sync.dma_start(rd[:].bitcast(I32), rd_words[0].rearrange("p c r -> p (c r)").bitcast(I32))
         load_scale_rows(nc.gpsimd, wrs_raw, wr_scales)
         load_scale_rows(nc.sync, rds, rd_scales)
         load_scale_rows(nc.sync, wbs_raw, wb_scales)
         nc.sync.dma_start(list3[:], offs3)
 
-        wa = [tile([P, R], U32, f"wa{z}") for z in range(2)]
-        was = [tile([P, R], U8, f"was{z}") for z in range(2)]
-        xg = [[tile([P, HALF], U16, f"xg{z}{h}") for h in range(2)] for z in range(2)]
-        cols = HALF // 16
-        nc.vector.tensor_copy(sg[0][:], xs[:].indirect(list1[:]))
-        nc.scalar.dma_start(sg[1][0:112, :].bitcast(I32), sg[0][16:P, :].bitcast(I32))
-        for z in range(2):
-            nc.scalar.copy(dealt(wa[z][:], 4), undealt(wa_raw[z][:], 4))
+        wa = [tile([P, R], U32, f"wa{z}") for z in range(PASSES)]
+        was = [tile([P, R], U8, f"was{z}") for z in range(PASSES)]
+        xg = [[tile([P, HALF], U16, f"xg{z}{h}") for h in range(2)] for z in range(PASSES)]
+        half_columns = HALF // ENTRIES
+        for t in SLICE_ORDER:
+            nc.vector.tensor_copy(was[0][:, t * P : (t + 1) * P], was_raw[:, 0, t:R:PACK])
+        deal(nc.vector.tensor_copy, was[1][:], was_raw[:, 1, :], 1)
+        for z in range(PASSES):
+            deal(nc.scalar.copy, wa[z][:], wa_raw[z][:], 4)
             for h in range(2):
-                nc.vector.tensor_copy(xg[z][h][:], xw[z][:].indirect(list1[:, h * cols : (h + 1) * cols]))
-                if z == 0:
-                    nc.vector.tensor_copy(dealt(was[h][:], 16), undealt(was_raw[:, h, :], 16))
+                entries = list1[:, h * half_columns : (h + 1) * half_columns]
+                nc.vector.tensor_copy(xg[z][h][:], xw[z][:].indirect(entries))
 
-        order = (0, 2, 1, 3)
         a_ps = [[ps.tile([P, HALF], F32, name=f"a{h}{t}", tag=f"bank{h}{t}") for t in range(PACK)] for h in range(2)]
         hid = [tile([P, J], F32, f"hid{t}") for t in range(PACK)]
-        for z in range(2):
+        for z in range(PASSES):
             for h in range(2):
-                for t in order:
+                for t in SLICE_ORDER:
                     nc.tensor.matmul_mx(
                         a_ps[h][t][:],
                         lhsT=wa[z][:, t * P : (t + 1) * P].bitcast(E4M3X4),
@@ -118,26 +132,26 @@ def tile_list_three_list_relay_pl_kernel(
                         rhs=xg[z][h][:].bitcast(E2M1X4),
                         rhs_scale=sg[z][:, h * HALF : (h + 1) * HALF],
                         start=(z == 0),
-                        stop=(z == 1),
+                        stop=(z == PASSES - 1),
                     )
         wr = tile([P, N], U16, "wr")
         wrs = tile([P, N], U8, "wrs")
         wb = tile([P, N], U16, "wb")
         wbs = tile([P, N], U8, "wbs")
-        nc.scalar.copy(dealt(wr[:], 8), undealt(wr_raw[:], 8))
-        nc.scalar.copy(dealt(wb[:], 8), undealt(wb_raw[:], 8))
-        nc.gpsimd.tensor_copy(dealt(wrs[:], 16), undealt(wrs_raw[:, 0, :], 16))
-        nc.gpsimd.tensor_copy(dealt(wbs[:], 16), undealt(wbs_raw[:, 0, :], 16))
+        deal(nc.scalar.copy, wr[:], wr_raw[:], 2)
+        deal(nc.scalar.copy, wb[:], wb_raw[:], 2)
+        deal(nc.gpsimd.tensor_copy, wrs[:], wrs_raw[:, 0, :], 1)
+        deal(nc.gpsimd.tensor_copy, wbs[:], wbs_raw[:, 0, :], 1)
         for h in range(2):
-            for t in order:
-                part = hid[t][:, h * HALF : (h + 1) * HALF]
-                if t < 2:
-                    nc.scalar.activation(part, a_ps[h][t][:], ACT.Relu)
+            for t in SLICE_ORDER:
+                relu_out = hid[t][:, h * HALF : (h + 1) * HALF]
+                if t in SCALAR_SLICES:
+                    nc.scalar.activation(relu_out, a_ps[h][t][:], ACT.Relu)
                 else:
-                    nc.vector.tensor_scalar_max(part, a_ps[h][t][:], 0.0)
+                    nc.vector.tensor_scalar_max(relu_out, a_ps[h][t][:], 0.0)
 
         q_ps = [ps.tile([P, S], F32, name=f"q{t}", tag=f"bank1{t}") for t in range(PACK)]
-        for t in order:
+        for t in SLICE_ORDER:
             nc.tensor.matmul_mx(
                 q_ps[t][:],
                 lhsT=wr[:, t * P : (t + 1) * P].bitcast(E2M1X4),
@@ -149,17 +163,14 @@ def tile_list_three_list_relay_pl_kernel(
             )
 
         hg = tile([P, PACK, I], F32, "hg")
-        for t in order:
-            if t < 2:
+        for t in SLICE_ORDER:
+            if t in SCALAR_SLICES:
                 nc.scalar.activation(hg[:, t, :], hid[t][:].indirect(list2[:]), ACT.Copy)
             else:
                 nc.vector.tensor_copy(hg[:, t, :], hid[t][:].indirect(list2[:]))
         hb = tile([P, I, PACK], BF16, "hb")
-        for copy, part in ((nc.vector.tensor_copy, slice(0, 176)), (nc.scalar.copy, slice(176, I))):
-            copy(
-                hb[:, part, :].rearrange("p (c i) t -> p c t i", i=4),
-                hg[:, :, part].rearrange("p t (c i) -> p c t i", i=4),
-            )
+        interleave(nc.vector.tensor_copy, hb[:, :VECTOR_COLUMNS, :], hg[:, :, :VECTOR_COLUMNS])
+        interleave(nc.scalar.copy, hb[:, VECTOR_COLUMNS:, :], hg[:, :, VECTOR_COLUMNS:])
         hq = tile([P, I], U32, "hq")
         hqs = tile([P, I], U8, "hqs")
         nc.vector.quantize_mx(hq[:].bitcast(E4M3X4), hqs[:], hb[:].rearrange("p c t -> p (c t)"))
@@ -181,40 +192,34 @@ def tile_list_three_list_relay_pl_kernel(
                 nc.vector.tensor_copy(pwin[t][:, :I], p_ps[t][:])
 
         y_rows = out_0.rearrange("(p t) s -> p t s", t=PACK)
-        codes = out_1[0].rearrange("p c r -> p (c r)").bitcast(I32)
+        y_codes = out_1[0].rearrange("p c r -> p (c r)").bitcast(I32)
         yq = tile([P, S], U32, "yq")
         yqs = tile([P, S], U8, "yqs")
-        chunks = ((0, 256, (1,)), (256, 128, ()), (384, 128, ()))
-        pending = []
-        for first, width, on_vector in chunks:
+
+        def quantise_and_store(span, yb):
+            nc.vector.quantize_mx(yq[:, span].bitcast(E4M3X4), yqs[:, span], yb[:].rearrange("p c t -> p (c t)"))
+            nc.sync.dma_start(y_codes[:, span], yq[:, span].bitcast(I32))
+
+        rounded = None
+        for first, width, vector_slices in CHUNKS:
             span = slice(first, first + width)
-            entries = list3[:, first // 16 : (first + width) // 16]
+            entries = list3[:, first // ENTRIES : (first + width) // ENTRIES]
             y = tile([P, PACK, width], F32, f"y{first}")
             pg = [tile([P, width], F32, f"pg{first}_{t}") for t in range(PACK)]
             for t in range(PACK):
-                if t in on_vector:
+                if t in vector_slices:
                     nc.vector.tensor_copy(pg[t][:], pwin[t][:].indirect(entries))
                 else:
                     nc.scalar.activation(pg[t][:], pwin[t][:].indirect(entries), ACT.Copy)
             for t in range(PACK):
                 nc.vector.tensor_tensor(y[:, t, :], pg[t][:], q_ps[t][:, span], MULT)
-                if t == 0:
-                    for step in pending:
-                        step()
-                    pending.clear()
+                if t == 0 and rounded is not None:
+                    quantise_and_store(*rounded)
             nc.sync.dma_start(y_rows[:, :, span], y[:])
             yb = tile([P, width, PACK], BF16, f"yb{first}")
-            nc.vector.tensor_copy(
-                yb[:].rearrange("p (c i) t -> p c t i", i=4), y[:].rearrange("p t (c i) -> p c t i", i=4)
-            )
-
-            def quantise(span=span, yb=yb):
-                nc.vector.quantize_mx(yq[:, span].bitcast(E4M3X4), yqs[:, span], yb[:].rearrange("p c t -> p (c t)"))
-                nc.sync.dma_start(codes[:, span], yq[:, span].bitcast(I32))
-
-            pending.append(quantise)
-        for step in pending:
-            step()
-        for q in range(4):
+            interleave(nc.vector.tensor_copy, yb[:], y[:])
+            rounded = (span, yb)
+        quantise_and_store(*rounded)
+        for q in range(QUADRANTS):
             queue = nc.sync if q % 2 == 0 else nc.scalar
             queue.dma_start(out_2[0, 4 * q : 4 * q + 4, :].bitcast(I32), yqs[32 * q : 32 * q + 4, :].bitcast(I32))

from contextlib import ExitStack

import concourse.mybir as mybir

K, T, J, I, R, S, L, N = 1024, 2048, 512, 256, 512, 512, 512, 512
FLOPS = 2 * (K * R * J + R * N * I + L * N * S)

F32 = mybir.dt.float32
BF16 = mybir.dt.bfloat16
I32 = mybir.dt.int32
U32 = mybir.dt.uint32
U16 = mybir.dt.uint16
U8 = mybir.dt.uint8
E4M3X4 = mybir.dt.float8_e4m3fn_x4
E2M1X4 = mybir.dt.float4_e2m1fn_x4
ACT = mybir.ActivationFunctionType
MULT = mybir.AluOpType.mult

P = 128
PACK = 4
PASSES = K // (P * PACK)
QUADRANTS = 4
ENTRIES = 16
LINE = 16
HALF = J // 2
SPARE = 16
SHIFT = 16
SLICE_ORDER = (0, 2, 1, 3)
SCALAR_SLICES = (0, 1)
VECTOR_COLUMNS = 176
CHUNKS = ((0, 256, (1,)), (256, 128, ()), (384, 128, ()))


def deal(copy, dealt, raw, element_bytes):
    run = LINE // element_bytes
    copy(
        dealt.rearrange("p (t b m) -> p b t m", t=PACK, m=run),
        raw.rearrange("p (b m t) -> p b t m", t=PACK, m=run),
    )


def interleave(copy, words, slices):
    copy(words.rearrange("p (c i) t -> p c t i", i=4), slices.rearrange("p t (c i) -> p c t i", i=4))


def tile_list_three_list_relay_pl_kernel(
    tc, xt_words, xt_scales, wa_words, wa_scales, wb_words, wb_scales, rd_words, rd_scales,
    wr_words, wr_scales, offs, offs2, offs3, out_0, out_1, out_2,
):
    nc = tc.nc
    with ExitStack() as ctx:
        sb = ctx.enter_context(tc.tile_pool(name="sb", bufs=1))
        ps = ctx.enter_context(tc.psum_pool(name="ps", bufs=1))

        def tile(shape, dtype, name):
            return sb.tile(shape, dtype, name=name, align_bytes=64)

        def load_scale_rows(queue, rows, scales):
            for q in range(QUADRANTS):
                queue.dma_start(
                    rows[32 * q : 32 * q + 4, :, :].bitcast(I32),
                    scales[:, 4 * q : 4 * q + 4, :].rearrange("z r c -> r z c").bitcast(I32),
                )

        list1 = sb.tile([P, J // ENTRIES], U16, name="list1")
        list2 = sb.tile([P, I // ENTRIES], U16, name="list2")
        list3 = sb.tile([P, S // ENTRIES], U16, name="list3")
        xw = [tile([P, T], U16, f"xw{z}") for z in range(PASSES)]
        xs = tile([P, T], U8, "xs")
        wa_raw = [tile([P, R], U32, f"wa_raw{z}") for z in range(PASSES)]
        was_raw = tile([P, PASSES, R], U8, "was_raw")
        rd = tile([P, S], U32, "rd")
        rds = tile([P, 1, S], U8, "rds")
        wr_raw = tile([P, N], U16, "wr_raw")
        wrs_raw = tile([P, 1, N], U8, "wrs_raw")
        wb_raw = tile([P, N], U16, "wb_raw")
        wbs_raw = tile([P, 1, N], U8, "wbs_raw")
        pwin = [tile([P, I + SPARE], F32, f"pwin{t}") for t in range(PACK)]

        sg = [tile([P, J], U8, f"sg{z}") for z in range(PASSES)]
        nc.gpsimd.memset(xs[:].bitcast(I32), 0)
        for rows in (was_raw, wrs_raw, rds, wbs_raw):
            nc.gpsimd.memset(rows[:].bitcast(I32), 0)
        nc.gpsimd.memset(sg[1][:].bitcast(I32), 0)
        zeros = tile([P, SPARE], F32, "zeros")
        nc.vector.memset(zeros[:], 0.0)
        for t in range(PACK):
            nc.scalar.copy(pwin[t][:, I:], zeros[:])

        nc.sync.dma_start(list1[:], offs)
        nc.sync.dma_start(list2[:], offs2)
        xs_rows = xt_scales.rearrange("z (q r) c -> r q z c", r=4).bitcast(I32)
        for r in range(4):
            nc.sync.dma_start(xs[r:P:SHIFT, :].bitcast(I32), xs_rows[r])
        nc.sync.dma_start(xw[0][:].bitcast(I32), xt_words[0].bitcast(I32))
        nc.sync.dma_start(wa_raw[0][:].bitcast(I32), wa_words[0].rearrange("p c r -> p (c r)").bitcast(I32))
        load_scale_rows(nc.sync, was_raw, wa_scales)
        nc.sync.dma_start(xw[1][:].bitcast(I32), xt_words[1].bitcast(I32))
        nc.sync.dma_start(wa_raw[1][:].bitcast(I32), wa_words[1].rearrange("p c r -> p (c r)").bitcast(I32))
        nc.sync.dma_start(wr_raw[:].bitcast(I32), wr_words[0].bitcast(I32))
        nc.sync.dma_start(wb_raw[:].bitcast(I32), wb_words[0].bitcast(I32))
        nc.vector.tensor_copy(sg[0][:], xs[:].indirect(list1[:]))
        nc.sync.dma_start(sg[1][0 : P - SHIFT, :].bitcast(I32), sg[0][SHIFT:P, :].bitcast(I32))
        nc.sync.dma_start(rd[:].bitcast(I32), rd_words[0].rearrange("p c r -> p (c r)").bitcast(I32))
        load_scale_rows(nc.gpsimd, wrs_raw, wr_scales)
        load_scale_rows(nc.sync, rds, rd_scales)
        load_scale_rows(nc.sync, wbs_raw, wb_scales)
        nc.sync.dma_start(list3[:], offs3)

        wa = [tile([P, R], U32, f"wa{z}") for z in range(PASSES)]
        was = [tile([P, R], U8, f"was{z}") for z in range(PASSES)]
        xg = [[tile([P, HALF], U16, f"xg{z}{h}") for h in range(2)] for z in range(PASSES)]
        half_columns = HALF // ENTRIES
        for t in SLICE_ORDER:
            nc.vector.tensor_copy(was[0][:, t * P : (t + 1) * P], was_raw[:, 0, t:R:PACK])
        deal(nc.vector.tensor_copy, was[1][:], was_raw[:, 1, :], 1)
        for z in range(PASSES):
            deal(nc.scalar.copy, wa[z][:], wa_raw[z][:], 4)
            for h in range(2):
                entries = list1[:, h * half_columns : (h + 1) * half_columns]
                nc.vector.tensor_copy(xg[z][h][:], xw[z][:].indirect(entries))

        a_ps = [[ps.tile([P, HALF], F32, name=f"a{h}{t}", tag=f"bank{h}{t}") for t in range(PACK)] for h in range(2)]
        hid = [tile([P, J], F32, f"hid{t}") for t in range(PACK)]
        for z in range(PASSES):
            for h in range(2):
                for t in SLICE_ORDER:
                    nc.tensor.matmul_mx(
                        a_ps[h][t][:],
                        lhsT=wa[z][:, t * P : (t + 1) * P].bitcast(E4M3X4),
                        lhsT_scale=was[z][:, t * P : (t + 1) * P],
                        rhs=xg[z][h][:].bitcast(E2M1X4),
                        rhs_scale=sg[z][:, h * HALF : (h + 1) * HALF],
                        start=(z == 0),
                        stop=(z == PASSES - 1),
                    )
        wr = tile([P, N], U16, "wr")
        wrs = tile([P, N], U8, "wrs")
        wb = tile([P, N], U16, "wb")
        wbs = tile([P, N], U8, "wbs")
        deal(nc.scalar.copy, wr[:], wr_raw[:], 2)
        deal(nc.scalar.copy, wb[:], wb_raw[:], 2)
        deal(nc.gpsimd.tensor_copy, wrs[:], wrs_raw[:, 0, :], 1)
        deal(nc.gpsimd.tensor_copy, wbs[:], wbs_raw[:, 0, :], 1)
        for h in range(2):
            for t in SLICE_ORDER:
                relu_out = hid[t][:, h * HALF : (h + 1) * HALF]
                if t in SCALAR_SLICES:
                    nc.scalar.activation(relu_out, a_ps[h][t][:], ACT.Relu)
                else:
                    nc.vector.tensor_scalar_max(relu_out, a_ps[h][t][:], 0.0)

        q_ps = [ps.tile([P, S], F32, name=f"q{t}", tag=f"bank1{t}") for t in range(PACK)]
        for t in SLICE_ORDER:
            nc.tensor.matmul_mx(
                q_ps[t][:],
                lhsT=wr[:, t * P : (t + 1) * P].bitcast(E2M1X4),
                lhsT_scale=wrs[:, t * P : (t + 1) * P],
                rhs=rd[:].bitcast(E4M3X4),
                rhs_scale=rds[:, 0, :],
                start=True,
                stop=True,
            )

        hg = tile([P, PACK, I], F32, "hg")
        for t in SLICE_ORDER:
            if t in SCALAR_SLICES:
                nc.scalar.activation(hg[:, t, :], hid[t][:].indirect(list2[:]), ACT.Copy)
            else:
                nc.vector.tensor_copy(hg[:, t, :], hid[t][:].indirect(list2[:]))
        hb = tile([P, I, PACK], BF16, "hb")
        interleave(nc.vector.tensor_copy, hb[:, :VECTOR_COLUMNS, :], hg[:, :, :VECTOR_COLUMNS])
        interleave(nc.scalar.copy, hb[:, VECTOR_COLUMNS:, :], hg[:, :, VECTOR_COLUMNS:])
        hq = tile([P, I], U32, "hq")
        hqs = tile([P, I], U8, "hqs")
        nc.vector.quantize_mx(hq[:].bitcast(E4M3X4), hqs[:], hb[:].rearrange("p c t -> p (c t)"))
        p_ps = [ps.tile([P, I], F32, name=f"p{t}", tag=f"bank0{t}") for t in range(PACK)]
        for t in range(PACK):
            nc.tensor.matmul_mx(
                p_ps[t][:],
                lhsT=wb[:, t * P : (t + 1) * P].bitcast(E2M1X4),
                lhsT_scale=wbs[:, t * P : (t + 1) * P],
                rhs=hq[:].bitcast(E4M3X4),
                rhs_scale=hqs[:],
                start=True,
                stop=True,
            )
        for t in range(PACK):
            if t % 2 == 0:
                nc.scalar.copy(pwin[t][:, :I], p_ps[t][:])
            else:
                nc.vector.tensor_copy(pwin[t][:, :I], p_ps[t][:])

        y_rows = out_0.rearrange("(p t) s -> p t s", t=PACK)
        y_codes = out_1[0].rearrange("p c r -> p (c r)").bitcast(I32)
        yq = tile([P, S], U32, "yq")
        yqs = tile([P, S], U8, "yqs")

        def quantise_and_store(span, yb):
            nc.vector.quantize_mx(yq[:, span].bitcast(E4M3X4), yqs[:, span], yb[:].rearrange("p c t -> p (c t)"))
            nc.sync.dma_start(y_codes[:, span], yq[:, span].bitcast(I32))

        rounded = None
        for first, width, vector_slices in CHUNKS:
            span = slice(first, first + width)
            entries = list3[:, first // ENTRIES : (first + width) // ENTRIES]
            y = tile([P, PACK, width], F32, f"y{first}")
            pg = [tile([P, width], F32, f"pg{first}_{t}") for t in range(PACK)]
            for t in range(PACK):
                if t in vector_slices:
                    nc.vector.tensor_copy(pg[t][:], pwin[t][:].indirect(entries))
                else:
                    nc.scalar.activation(pg[t][:], pwin[t][:].indirect(entries), ACT.Copy)
            for t in range(PACK):
                nc.vector.tensor_tensor(y[:, t, :], pg[t][:], q_ps[t][:, span], MULT)
                if t == 0 and rounded is not None:
                    quantise_and_store(*rounded)
            nc.sync.dma_start(y_rows[:, :, span], y[:])
            yb = tile([P, width, PACK], BF16, f"yb{first}")
            interleave(nc.vector.tensor_copy, yb[:], y[:])
            rounded = (span, yb)
        quantise_and_store(*rounded)
        for q in range(QUADRANTS):
            queue = nc.sync if q % 2 == 0 else nc.scalar
            queue.dma_start(out_2[0, 4 * q : 4 * q + 4, :].bitcast(I32), yqs[32 * q : 32 * q + 4, :].bitcast(I32))
